import numpy as np
import ml_dtypes


def mxq(x, axis, fmt="e4m3"):
    dtype, down = {"e4m3": (ml_dtypes.float8_e4m3fn, 7), "e5m2": (ml_dtypes.float8_e5m2, 14)}[fmt]
    v = np.moveaxis(np.asarray(x, np.float32).astype(ml_dtypes.bfloat16).astype(np.float64), axis, -1)
    blocks = v.reshape(v.shape[:-1] + (-1, 32))
    amax = np.abs(blocks).max(-1, keepdims=True)
    byte = np.maximum(np.where(amax > 0, np.frexp(amax)[1] - 1 + 127, 0) - down, 1)
    scale = np.exp2(byte - 127.0)
    codes = (blocks / scale).astype(np.float32).astype(dtype).astype(np.float64)
    return np.moveaxis((codes * scale).reshape(v.shape), -1, axis)


WIDE = False


def mx_kscale(k):
    if not WIDE:
        return np.ones(k)
    levels = np.array([10, -10, 5, -5, 0])
    if k % 512:
        return np.exp2(np.random.permutation(np.resize(levels, k // 32))).repeat(32)
    a = np.empty((k // 512, 16))
    for p in range(k // 512):
        a[p, :8] = np.random.permutation(np.resize(levels, 8))
        for g in range(8):
            far = levels[np.abs(levels - a[p, g]) >= 10]
            a[p, g + 8] = far[np.random.randint(len(far))]
    return np.exp2(a.ravel()).repeat(32)


def f64(x):
    return np.asarray(x).astype(np.float64)


def striped(idx):
    return np.tile(idx.reshape(-1, 16).T, (8, 1)).astype(np.uint16)


def unstriped(offs):
    return offs[:16].T.reshape(-1).astype(np.int64)


def pack_weight(w):
    k, n = w.shape
    w = f64(np.asarray(w, np.float32).astype(ml_dtypes.bfloat16)).reshape(k // 32, 32, n)
    amax = np.abs(w).max(1)
    byte = np.clip(np.where(amax > 0, np.frexp(amax)[1] - 1 + 127 - 7, 1), 1, 254)
    scaled = (w * np.exp2(127.0 - byte)[:, None, :]).reshape(k, n).astype(np.float32)
    words = np.ascontiguousarray(scaled.reshape(k // 512, 128, 4, n).transpose(0, 1, 3, 2)).astype(ml_dtypes.float8_e4m3fn).view(np.uint8)
    return words, np.ascontiguousarray(byte.astype(np.uint8).reshape(k // 512, 16, n))


def unpack_weight(words, scales):
    g, p, n, _ = words.shape
    vals = np.ascontiguousarray(words).view(ml_dtypes.float8_e4m3fn).astype(np.float64) * np.repeat(np.exp2(scales.astype(np.float64) - 127.0), 8, axis=1)[..., None]
    return vals.transpose(0, 1, 3, 2).reshape(g * 512, n)


def sigmoid(v):
    return 1.0 / (1.0 + np.exp(-np.maximum(v, -700.0)))


K, T, S, D, N, H = 1024, 2048, 512, 4, 256, 512


def setup_inputs():
    n = np.random.standard_normal
    s = mx_kscale(K)[:, None]
    u = mx_kscale(H)
    packed_xT = pack_weight(n((K, T)) * s)
    return {
        "x_words": packed_xT[0],
        "x_scales": packed_xT[1],
        "w1": (n((K, H)) / np.sqrt(K) / s).astype(np.float32),
        "w2": (n((K, H)) / np.sqrt(K) / s).astype(np.float32),
        "unit": (np.random.uniform(0.6, 1.4, (H, 1)) * u[:, None]).astype(np.float32),
        "w3": (n((H, N)) / np.sqrt(H) / u[:, None]).astype(np.float32),
        "offs": striped(np.random.permutation(T)[:S]),
        "pf": striped(np.random.permutation(S)),
    }


def reference(x_words, x_scales, w1, w2, unit, w3, offs, pf):
    xq = unpack_weight(x_words, x_scales)[:, unstriped(offs)]
    fr = mxq(f64(w2), 0, "e4m3").T @ xq
    freq = np.log(np.exp(fr) + 1.0)
    rc = mxq(f64(w1), 0, "e4m3").T @ xq
    recy = np.log(np.exp(rc) + 1.0)
    util = freq / (recy + 0.4)
    vict = util.reshape(len(util), -1, D).min(axis=2)
    marg = util - np.repeat(vict, D, axis=1)
    upf = util[:, unstriped(pf)]
    adm = sigmoid(1.5 * (upf - util))
    hid = f64(unit) * (marg * (-1.0 * adm + 1.0) + adm * upf)
    return mxq(f64(w3), 0, "e4m3").T @ mxq(hid, 0, "e4m3")

@@ -1,0 +1,269 @@
+import math
+from contextlib import ExitStack
+
+import concourse.mybir as mybir
+
+K, T, S, D, N, H = 1024, 2048, 512, 4, 256, 512
+FLOPS = 2 * K * H * S * 2 + 2 * H * N * S
+
+F32 = mybir.dt.float32
+BF16 = mybir.dt.bfloat16
+I32 = mybir.dt.int32
+U32 = mybir.dt.uint32
+U16 = mybir.dt.uint16
+U8 = mybir.dt.uint8
+FP8X4 = mybir.dt.float8_e4m3fn_x4
+ALU = mybir.AluOpType
+ACT = mybir.ActivationFunctionType
+
+P = 128
+PACK = 4
+PASSES = K // (P * PACK)
+EXP_CAP = math.exp(32.0)
+OUT_CHUNK = 256
+
+
+def tile_picked_ycachep_adm_p_kernel(
+    tc, x_words, x_scales, w1, w2, unit, w3, offs, pf, out
+):
+    nc = tc.nc
+    with ExitStack() as ctx:
+        keep = ctx.enter_context(tc.tile_pool(name="keep", bufs=1))
+        psum = ctx.enter_context(tc.psum_pool(name="psum", bufs=1))
+
+        def sb(name, shape, dtype, tag=None):
+            return keep.tile(shape, dtype, name=name, tag=tag or name, align_bytes=64)
+
+        offs_sb = keep.tile([P, S // 16], U16, name="offs_sb")
+        pf_sb = keep.tile([P, S // 16], U16, name="pf_sb")
+        nc.sync.dma_start(offs_sb[:], offs)
+
+        xs_table = sb("xs_table", [P, T], U8)
+        nc.vector.memset(xs_table[:].bitcast(I32), 0)
+        for q in range(4):
+            nc.scalar.dma_start(
+                xs_table[32 * q : 32 * q + 4 * PASSES, :].bitcast(I32),
+                x_scales[:, 4 * q : 4 * q + 4, :].bitcast(I32),
+            )
+
+        def load_weight(name, w, o, c0, c1):
+            raw = sb(f"{name}_raw{o}_{c0}", [P, PACK, c1 - c0], F32)
+            nc.sync.dma_start(raw[:], w[512 * o : 512 * (o + 1), c0:c1].rearrange("(p j) c -> p j c", j=PACK))
+            return raw
+
+        def load_words(o):
+            tab = sb(f"xw_table{o}", [P, T], I32)
+            nc.sync.dma_start(tab[:], x_words[o].rearrange("p c r -> p (c r)").bitcast(I32))
+            return tab
+
+        xw_table = [load_words(0)]
+        w1a = [load_weight("w1", w1, 0, 0, H)]
+        w2a = [load_weight("w2", w2, 0, 0, H)]
+        xw_table.append(load_words(1))
+        w1b = [load_weight("w1", w1, 1, 0, H)]
+        w2b = [load_weight("w2", w2, 1, c, c + H // 2) for c in (0, H // 2)]
+        nc.sync.dma_start(pf_sb[:], pf)
+        unit_sb = sb("unit_sb", [P, PACK], F32)
+        nc.sync.dma_start(unit_sb[:], unit.rearrange("(p t) one -> p (t one)", t=PACK))
+        w3_raw = load_weight("w3", w3, 0, 0, N)
+
+        def round_first_weight(name, raws, copy):
+            grouped = sb(f"{name}_bf", [P, PACK, P, PACK], BF16)
+            width = P // len(raws)
+            for i, raw in enumerate(raws):
+                copy(
+                    grouped[:, :, width * i : width * (i + 1), :].rearrange("p t m j -> p m t j"),
+                    raw[:].rearrange("p j (m t) -> p m t j", t=PACK),
+                )
+            return grouped
+
+        def quantize_first_weight(name, grouped, pieces):
+            codes = sb(f"{name}_codes", [P, H], U32)
+            scales = sb(f"{name}_scales", [P, H], U8)
+            flat = grouped[:].rearrange("p t m j -> p (t m j)")
+            width = H // pieces
+            for i in range(pieces):
+                cols = slice(width * i, width * (i + 1))
+                nc.vector.quantize_mx(
+                    out=codes[:, cols].bitcast(FP8X4),
+                    scales=scales[:, cols],
+                    in_=flat[:, PACK * width * i : PACK * width * (i + 1)],
+                )
+            return codes, scales
+
+        def gather_words(o):
+            g = sb(f"xw{o}", [P, S], U32)
+            nc.vector.tensor_copy(g[:], xw_table[o][:].bitcast(U32).indirect(offs_sb[:]))
+            return g
+
+        rc = [psum.tile([P, S], F32, name=f"rc{t}", tag=f"rc{t}") for t in range(PACK)]
+        fr = [psum.tile([P, S], F32, name=f"fr{t}", tag=f"fr{t}") for t in range(PACK)]
+
+        def first_pass(banks, wq, o):
+            for t in range(PACK):
+                cols = slice(P * t, P * (t + 1))
+                nc.tensor.matmul_mx(
+                    out=banks[t][:],
+                    lhsT=wq[0][:, cols].bitcast(FP8X4),
+                    lhsT_scale=wq[1][:, cols],
+                    rhs=xw[o][:].bitcast(FP8X4),
+                    rhs_scale=xs[4 * o : P, :],
+                    start=(o == 0),
+                    stop=(o == PASSES - 1),
+                )
+
+        xw = [gather_words(0)]
+        xs = sb("xs", [P, S], U8)
+        nc.vector.tensor_copy(xs[:], xs_table[:].indirect(offs_sb[:]))
+        w1a_q = quantize_first_weight("w1a", round_first_weight("w1a", w1a, nc.scalar.copy), 1)
+        first_pass(rc, w1a_q, 0)
+        w2a_q = quantize_first_weight("w2a", round_first_weight("w2a", w2a, nc.scalar.copy), 1)
+        first_pass(fr, w2a_q, 0)
+        xw.append(gather_words(1))
+        w1b_q = quantize_first_weight("w1b", round_first_weight("w1b", w1b, nc.vector.tensor_copy), PACK)
+        first_pass(rc, w1b_q, 1)
+        w2b_q = quantize_first_weight("w2b", round_first_weight("w2b", w2b, nc.vector.tensor_copy), PACK)
+        first_pass(fr, w2b_q, 1)
+
+        def plane(tile, t):
+            return tile[:, S * t : S * (t + 1)]
+
+        e_rc = sb("e_rc", [P, PACK * S], F32)
+        ec_rc = sb("ec_rc", [P, PACK * S], F32)
+        for t in range(PACK):
+            nc.scalar.activation(plane(e_rc, t), rc[t][:], ACT.Exp)
+        e_fr = sb("e_fr", [P, PACK * S], F32, tag="before_ln")
+        ec_fr = sb("ec_fr", [P, PACK * S], F32)
+        for t in range(PACK):
+            nc.scalar.activation(plane(e_fr, t), fr[t][:], ACT.Exp)
+        nc.vector.tensor_scalar_min(ec_rc[:], e_rc[:], EXP_CAP)
+        for t in range(PACK):
+            nc.vector.tensor_scalar_min(plane(ec_fr, t), plane(e_fr, t), EXP_CAP)
+
+        logs = sb("logs", [P, 2 * PACK * S], F32, tag="before_ln")
+        recy = sb("recy", [P, PACK * S], F32, tag="before_exp")
+        freq = sb("freq", [P, PACK * S], F32)
+        for t in range(PACK):
+            nc.scalar.activation(plane(logs, t), plane(ec_rc, t), ACT.Ln, bias=1.0)
+            nc.vector.tensor_tensor(plane(recy, t), rc[t][:], plane(logs, t), ALU.max)
+        for t in range(PACK):
+            nc.scalar.activation(plane(logs, PACK + t), plane(ec_fr, t), ACT.Ln, bias=1.0)
+            nc.vector.tensor_tensor(plane(freq, t), fr[t][:], plane(logs, PACK + t), ALU.max)
+        l_den = sb("l_den", [P, PACK * S], F32)
+        for t in range(PACK):
+            nc.scalar.activation(plane(l_den, t), plane(recy, t), ACT.Ln, bias=0.4)
+
+        w3_bf = sb("w3_bf", [P, N, PACK], BF16)
+        nc.vector.tensor_copy(w3_bf[:], w3_raw[:].rearrange("p j n -> p n j"))
+        w3_codes = sb("w3_codes", [P, N], U32)
+        w3_scales = sb("w3_scales", [P, N], U8)
+        nc.vector.quantize_mx(
+            out=w3_codes[:].bitcast(FP8X4), scales=w3_scales[:], in_=w3_bf[:].rearrange("p n j -> p (n j)")
+        )
+        half_unit = sb("half_unit", [P, PACK], F32)
+        nc.vector.tensor_scalar_mul(half_unit[:], unit_sb[:], 0.5)
+
+        inv = sb("inv", [P, PACK * S], F32, tag="before_exp")
+        upf_u = sb("upf_u", [P, PACK, S], F32)
+        lost = sb("lost", [P, PACK, S], F32)
+        util, upf, vict, diff, th, gap = {}, {}, {}, {}, {}, {}
+
+        def reciprocal(t):
+            nc.scalar.activation(plane(inv, t), plane(l_den, t), ACT.Exp, scale=-1.0)
+
+        def utility(t):
+            util[t] = sb(f"util{t}", [P, S], F32)
+            nc.vector.tensor_tensor(util[t][:], plane(freq, t), plane(inv, t), ALU.mult)
+
+        def fetch(t):
+            upf[t] = sb(f"upf{t}", [P, S], F32)
+            for h in range(2):
+                nc.scalar.activation(
+                    upf[t][:, 256 * h : 256 * (h + 1)], util[t][:].indirect(pf_sb[:, 16 * h : 16 * (h + 1)]), ACT.Copy
+                )
+
+        def victim(t):
+            pairs = sb(f"pairs{t}", [P, S // 2], F32)
+            uv = util[t][:].rearrange("p (v e) -> p v e", e=2)
+            nc.vector.tensor_tensor(pairs[:], uv[:, :, 0], uv[:, :, 1], ALU.min)
+            low = sb(f"low{t}", [P, S // D], F32)
+            pv = pairs[:].rearrange("p (v e) -> p v e", e=2)
+            nc.vector.tensor_tensor(low[:], pv[:, :, 0], pv[:, :, 1], ALU.min)
+            vict[t] = sb(f"vict{t}", [P, S // D], F32)
+            nc.scalar.activation(vict[t][:], low[:], ACT.Copy, scale=half_unit[:, t : t + 1])
+
+        def difference(t):
+            diff[t] = sb(f"diff{t}", [P, S], F32)
+            nc.vector.tensor_tensor(diff[t][:], upf[t][:], util[t][:], ALU.subtract)
+
+        def gate(t):
+            th[t] = sb(f"th{t}", [P, S], F32)
+            nc.scalar.activation(th[t][:], diff[t][:], ACT.Tanh, scale=0.75)
+
+        def gapf(t):
+            gap[t] = sb(f"gap{t}", [P, S // D, D], F32)
+            nc.vector.scalar_tensor_tensor(
+                gap[t][:],
+                diff[t][:].rearrange("p (v d) -> p v d", d=D),
+                half_unit[:, t : t + 1],
+                vict[t][:].unsqueeze(2).to_broadcast([P, S // D, D]),
+                ALU.mult,
+                ALU.add,
+            )
+
+        def scale_upf(t):
+            nc.scalar.activation(upf_u[:, t, :], upf[t][:], ACT.Copy, scale=unit_sb[:, t : t + 1])
+
+        def loss(t):
+            nc.vector.scalar_tensor_tensor(
+                lost[:, t, :], th[t][:], -1.0, gap[t][:].rearrange("p v d -> p (v d)"), ALU.add, ALU.mult
+            )
+
+        reciprocal(0)
+        for step in range(PACK + 2):
+            if step + 1 < PACK:
+                reciprocal(step + 1)
+            if step < PACK:
+                utility(step)
+                fetch(step)
+                victim(step)
+            if 0 <= step - 1 < PACK:
+                difference(step - 1)
+                gate(step - 1)
+                gapf(step - 1)
+            if 0 <= step - 2 < PACK:
+                loss(step - 2)
+                scale_upf(step - 2)
+
+        for c in range(S // OUT_CHUNK):
+            cols = slice(OUT_CHUNK * c, OUT_CHUNK * (c + 1))
+            hid_bf = sb(f"hid_bf{c}", [P, OUT_CHUNK, PACK], BF16)
+            nc.vector.tensor_tensor(
+                hid_bf[:].rearrange("p (c i) t -> p c t i", i=4),
+                upf_u[:, :, cols].rearrange("p t (c i) -> p c t i", i=4),
+                lost[:, :, cols].rearrange("p t (c i) -> p c t i", i=4),
+                ALU.add,
+            )
+            h_codes = sb(f"h_codes{c}", [P, OUT_CHUNK], U32)
+            h_scales = sb(f"h_scales{c}", [P, OUT_CHUNK], U8)
+            nc.vector.quantize_mx(
+                out=h_codes[:].bitcast(FP8X4), scales=h_scales[:], in_=hid_bf[:].rearrange("p j t -> p (j t)")
+            )
+            for m in range(N // P):
+                rows = slice(P * m, P * (m + 1))
+                acc = psum.tile([P, OUT_CHUNK], F32, name=f"o{c}{m}", tag=f"rc{2 * c + m}")
+                nc.tensor.matmul_mx(
+                    out=acc[:],
+                    lhsT=w3_codes[:, rows].bitcast(FP8X4),
+                    lhsT_scale=w3_scales[:, rows],
+                    rhs=h_codes[:].bitcast(FP8X4),
+                    rhs_scale=h_scales[:],
+                    start=True,
+                    stop=True,
+                )
+                res = sb(f"res{c}{m}", [P, OUT_CHUNK], F32)
+                if c == S // OUT_CHUNK - 1 and m == 1:
+                    nc.vector.tensor_copy(res[:], acc[:])
+                else:
+                    nc.scalar.copy(res[:], acc[:])
+                nc.sync.dma_start(out[rows, cols], res[:])

@@ -37,9 +37,12 @@ def tile_picked_ycachep_adm_p_kernel(
         offs_sb = keep.tile([P, S // 16], U16, name="offs_sb")
         pf_sb = keep.tile([P, S // 16], U16, name="pf_sb")
         nc.sync.dma_start(offs_sb[:], offs)
+        nc.sync.dma_start(pf_sb[:], pf)
+        unit_sb = sb("unit_sb", [P, PACK], F32)
+        nc.sync.dma_start(unit_sb[:], unit.rearrange("(p t) one -> p (t one)", t=PACK))
 
         xs_table = sb("xs_table", [P, T], U8)
-        nc.vector.memset(xs_table[:].bitcast(I32), 0)
+        nc.gpsimd.memset(xs_table[:].bitcast(I32), 0)
         for q in range(4):
             nc.scalar.dma_start(
                 xs_table[32 * q : 32 * q + 4 * PASSES, :].bitcast(I32),
@@ -56,15 +59,11 @@ def tile_picked_ycachep_adm_p_kernel(
             nc.sync.dma_start(tab[:], x_words[o].rearrange("p c r -> p (c r)").bitcast(I32))
             return tab
 
-        xw_table = [load_words(0)]
         w1a = [load_weight("w1", w1, 0, 0, H)]
         w2a = [load_weight("w2", w2, 0, 0, H)]
-        xw_table.append(load_words(1))
-        w1b = [load_weight("w1", w1, 1, 0, H)]
+        xw_table = [load_words(o) for o in range(PASSES)]
+        w1b = [load_weight("w1", w1, 1, c, c + H // 2) for c in (0, H // 2)]
         w2b = [load_weight("w2", w2, 1, c, c + H // 2) for c in (0, H // 2)]
-        nc.sync.dma_start(pf_sb[:], pf)
-        unit_sb = sb("unit_sb", [P, PACK], F32)
-        nc.sync.dma_start(unit_sb[:], unit.rearrange("(p t) one -> p (t one)", t=PACK))
         w3_raw = load_weight("w3", w3, 0, 0, N)
 
         def round_first_weight(name, raws, copy):
@@ -72,8 +71,8 @@ def tile_picked_ycachep_adm_p_kernel(
             width = P // len(raws)
             for i, raw in enumerate(raws):
                 copy(
-                    grouped[:, :, width * i : width * (i + 1), :].rearrange("p t m j -> p m t j"),
-                    raw[:].rearrange("p j (m t) -> p m t j", t=PACK),
+                    grouped[:, :, width * i : width * (i + 1), :].rearrange("p t m j -> p m j t"),
+                    raw[:].rearrange("p j (m t) -> p m j t", t=PACK),
                 )
             return grouped
 
@@ -112,12 +111,12 @@ def tile_picked_ycachep_adm_p_kernel(
                     stop=(o == PASSES - 1),
                 )
 
-        xw = [gather_words(0)]
         xs = sb("xs", [P, S], U8)
         nc.vector.tensor_copy(xs[:], xs_table[:].indirect(offs_sb[:]))
         w1a_q = quantize_first_weight("w1a", round_first_weight("w1a", w1a, nc.scalar.copy), 1)
-        first_pass(rc, w1a_q, 0)
         w2a_q = quantize_first_weight("w2a", round_first_weight("w2a", w2a, nc.scalar.copy), 1)
+        xw = [gather_words(0)]
+        first_pass(rc, w1a_q, 0)
         first_pass(fr, w2a_q, 0)
         xw.append(gather_words(1))
         w1b_q = quantize_first_weight("w1b", round_first_weight("w1b", w1b, nc.vector.tensor_copy), PACK)
@@ -129,7 +128,7 @@ def tile_picked_ycachep_adm_p_kernel(
             return tile[:, S * t : S * (t + 1)]
 
         e_rc = sb("e_rc", [P, PACK * S], F32)
-        ec_rc = sb("ec_rc", [P, PACK * S], F32)
+        ec_rc = sb("ec_rc", [P, PACK * S], F32, tag="w2b_bf")
         for t in range(PACK):
             nc.scalar.activation(plane(e_rc, t), rc[t][:], ACT.Exp)
         e_fr = sb("e_fr", [P, PACK * S], F32, tag="before_ln")
@@ -166,7 +165,7 @@ def tile_picked_ycachep_adm_p_kernel(
         inv = sb("inv", [P, PACK * S], F32, tag="before_exp")
         upf_u = sb("upf_u", [P, PACK, S], F32)
         lost = sb("lost", [P, PACK, S], F32)
-        util, upf, vict, diff, th, gap = {}, {}, {}, {}, {}, {}
+        util, upf, pairs, vict, diff, th, gap = {}, {}, {}, {}, {}, {}, {}
 
         def reciprocal(t):
             nc.scalar.activation(plane(inv, t), plane(l_den, t), ACT.Exp, scale=-1.0)
@@ -182,12 +181,14 @@ def tile_picked_ycachep_adm_p_kernel(
                     upf[t][:, 256 * h : 256 * (h + 1)], util[t][:].indirect(pf_sb[:, 16 * h : 16 * (h + 1)]), ACT.Copy
                 )
 
-        def victim(t):
-            pairs = sb(f"pairs{t}", [P, S // 2], F32)
+        def pair_min(t):
+            pairs[t] = sb(f"pairs{t}", [P, S // 2], F32)
             uv = util[t][:].rearrange("p (v e) -> p v e", e=2)
-            nc.vector.tensor_tensor(pairs[:], uv[:, :, 0], uv[:, :, 1], ALU.min)
+            nc.vector.tensor_tensor(pairs[t][:], uv[:, :, 0], uv[:, :, 1], ALU.min)
+
+        def victim(t):
             low = sb(f"low{t}", [P, S // D], F32)
-            pv = pairs[:].rearrange("p (v e) -> p v e", e=2)
+            pv = pairs[t][:].rearrange("p (v e) -> p v e", e=2)
             nc.vector.tensor_tensor(low[:], pv[:, :, 0], pv[:, :, 1], ALU.min)
             vict[t] = sb(f"vict{t}", [P, S // D], F32)
             nc.scalar.activation(vict[t][:], low[:], ACT.Copy, scale=half_unit[:, t : t + 1])
@@ -214,44 +215,61 @@ def tile_picked_ycachep_adm_p_kernel(
         def scale_upf(t):
             nc.scalar.activation(upf_u[:, t, :], upf[t][:], ACT.Copy, scale=unit_sb[:, t : t + 1])
 
-        def loss(t):
+        def loss(t, cols):
             nc.vector.scalar_tensor_tensor(
-                lost[:, t, :], th[t][:], -1.0, gap[t][:].rearrange("p v d -> p (v d)"), ALU.add, ALU.mult
+                lost[:, t, cols], th[t][:, cols], -1.0, gap[t][:].rearrange("p v d -> p (v d)")[:, cols], ALU.add, ALU.mult
             )
 
+        chunks = [slice(0, 256), slice(256, 384), slice(384, 512)]
         reciprocal(0)
-        for step in range(PACK + 2):
-            if step + 1 < PACK:
-                reciprocal(step + 1)
-            if step < PACK:
-                utility(step)
-                fetch(step)
-                victim(step)
-            if 0 <= step - 1 < PACK:
-                difference(step - 1)
-                gate(step - 1)
-                gapf(step - 1)
-            if 0 <= step - 2 < PACK:
-                loss(step - 2)
-                scale_upf(step - 2)
+        reciprocal(1)
+        utility(0)
+        fetch(0)
+        for t in range(PACK):
+            if t + 2 < PACK:
+                reciprocal(t + 2)
+            if t + 1 < PACK:
+                utility(t + 1)
+                fetch(t + 1)
+            pair_min(t)
+            if t > 0:
+                gapf(t - 1)
+            victim(t)
+            if t > 1:
+                loss(t - 2, slice(0, S))
+            difference(t)
+            gate(t)
+            if t > 0:
+                scale_upf(t - 1)
+        loss(PACK - 2, slice(0, S))
+        gapf(PACK - 1)
+        scale_upf(PACK - 1)
+        loss(PACK - 1, slice(0, 256))
+        loss(PACK - 1, slice(256, 512))
 
-        for c in range(S // OUT_CHUNK):
-            cols = slice(OUT_CHUNK * c, OUT_CHUNK * (c + 1))
-            hid_bf = sb(f"hid_bf{c}", [P, OUT_CHUNK, PACK], BF16)
+        hid = {}
+
+        def combine(c):
+            cols = chunks[c]
+            hid[c] = sb(f"hid_bf{c}", [P, cols.stop - cols.start, PACK], BF16)
             nc.vector.tensor_tensor(
-                hid_bf[:].rearrange("p (c i) t -> p c t i", i=4),
+                hid[c][:].rearrange("p (c i) t -> p c t i", i=4),
                 upf_u[:, :, cols].rearrange("p t (c i) -> p c t i", i=4),
                 lost[:, :, cols].rearrange("p t (c i) -> p c t i", i=4),
                 ALU.add,
             )
-            h_codes = sb(f"h_codes{c}", [P, OUT_CHUNK], U32)
-            h_scales = sb(f"h_scales{c}", [P, OUT_CHUNK], U8)
+
+        def finish(c):
+            cols = chunks[c]
+            width = cols.stop - cols.start
+            h_codes = sb(f"h_codes{c}", [P, width], U32)
+            h_scales = sb(f"h_scales{c}", [P, width], U8)
             nc.vector.quantize_mx(
-                out=h_codes[:].bitcast(FP8X4), scales=h_scales[:], in_=hid_bf[:].rearrange("p j t -> p (j t)")
+                out=h_codes[:].bitcast(FP8X4), scales=h_scales[:], in_=hid[c][:].rearrange("p j t -> p (j t)")
             )
             for m in range(N // P):
                 rows = slice(P * m, P * (m + 1))
-                acc = psum.tile([P, OUT_CHUNK], F32, name=f"o{c}{m}", tag=f"rc{2 * c + m}")
+                acc = psum.tile([P, width], F32, name=f"o{c}{m}", tag=("rc", "fr")[m] + str(c))
                 nc.tensor.matmul_mx(
                     out=acc[:],
                     lhsT=w3_codes[:, rows].bitcast(FP8X4),
@@ -261,9 +279,16 @@ def tile_picked_ycachep_adm_p_kernel(
                     start=True,
                     stop=True,
                 )
-                res = sb(f"res{c}{m}", [P, OUT_CHUNK], F32)
-                if c == S // OUT_CHUNK - 1 and m == 1:
+                res = sb(f"res{c}{m}", [P, width], F32)
+                if c == len(chunks) - 1 and m == 1:
                     nc.vector.tensor_copy(res[:], acc[:])
+                    nc.sync.dma_start(out[rows, cols], res[:])
                 else:
                     nc.scalar.copy(res[:], acc[:])
-                nc.sync.dma_start(out[rows, cols], res[:])
+                    (nc.scalar if c == len(chunks) - 1 else nc.sync).dma_start(out[rows, cols], res[:])
+
+        combine(0)
+        for c in range(len(chunks)):
+            if c + 1 < len(chunks):
+                combine(c + 1)
+            finish(c)

@@ -20,7 +20,9 @@ P = 128
 PACK = 4
 PASSES = K // (P * PACK)
 EXP_CAP = math.exp(32.0)
-OUT_CHUNK = 256
+SHIFT = 0.4
+EXP_SHIFT = math.exp(SHIFT)
+DIV = 256
 
 
 def tile_picked_ycachep_adm_p_kernel(
@@ -139,18 +141,27 @@ def tile_picked_ycachep_adm_p_kernel(
         for t in range(PACK):
             nc.vector.tensor_scalar_min(plane(ec_fr, t), plane(e_fr, t), EXP_CAP)
 
+        den_head = sb("den_head", [P, DIV], F32)
         logs = sb("logs", [P, 2 * PACK * S], F32, tag="before_ln")
         recy = sb("recy", [P, PACK * S], F32, tag="before_exp")
         freq = sb("freq", [P, PACK * S], F32)
         for t in range(PACK):
-            nc.scalar.activation(plane(logs, t), plane(ec_rc, t), ACT.Ln, bias=1.0)
-            nc.vector.tensor_tensor(plane(recy, t), rc[t][:], plane(logs, t), ALU.max)
+            nc.scalar.activation(plane(logs, t), plane(ec_rc, t), ACT.Ln, scale=EXP_SHIFT, bias=EXP_SHIFT)
+            if t == 0:
+                nc.vector.scalar_tensor_tensor(den_head[:], rc[0][:, :DIV], SHIFT, logs[:, :DIV], ALU.add, ALU.max)
+            lo = DIV if t == 0 else 0
+            nc.vector.scalar_tensor_tensor(
+                plane(recy, t)[:, lo:], rc[t][:, lo:], SHIFT, plane(logs, t)[:, lo:], ALU.add, ALU.max
+            )
         for t in range(PACK):
             nc.scalar.activation(plane(logs, PACK + t), plane(ec_fr, t), ACT.Ln, bias=1.0)
             nc.vector.tensor_tensor(plane(freq, t), fr[t][:], plane(logs, PACK + t), ALU.max)
         l_den = sb("l_den", [P, PACK * S], F32)
         for t in range(PACK):
-            nc.scalar.activation(plane(l_den, t), plane(recy, t), ACT.Ln, bias=0.4)
+            lo = DIV if t == 0 else 0
+            nc.scalar.activation(plane(l_den, t)[:, lo:], plane(recy, t)[:, lo:], ACT.Ln)
+        inv_head = sb("inv_head", [P, DIV], F32, tag="before_ln")
+        nc.vector.reciprocal(inv_head[:], den_head[:])
 
         w3_bf = sb("w3_bf", [P, N, PACK], BF16)
         nc.vector.tensor_copy(w3_bf[:], w3_raw[:].rearrange("p j n -> p n j"))
@@ -168,11 +179,15 @@ def tile_picked_ycachep_adm_p_kernel(
         util, upf, pairs, vict, diff, th, gap = {}, {}, {}, {}, {}, {}, {}
 
         def reciprocal(t):
-            nc.scalar.activation(plane(inv, t), plane(l_den, t), ACT.Exp, scale=-1.0)
+            lo = DIV if t == 0 else 0
+            nc.scalar.activation(plane(inv, t)[:, lo:], plane(l_den, t)[:, lo:], ACT.Exp, scale=-1.0)
 
         def utility(t):
             util[t] = sb(f"util{t}", [P, S], F32)
-            nc.vector.tensor_tensor(util[t][:], plane(freq, t), plane(inv, t), ALU.mult)
+            lo = DIV if t == 0 else 0
+            if t == 0:
+                nc.vector.tensor_tensor(util[t][:, :DIV], freq[:, :DIV], inv_head[:], ALU.mult)
+            nc.vector.tensor_tensor(util[t][:, lo:], plane(freq, t)[:, lo:], plane(inv, t)[:, lo:], ALU.mult)
 
         def fetch(t):
             upf[t] = sb(f"upf{t}", [P, S], F32)

import math
from contextlib import ExitStack

import concourse.mybir as mybir

K, T, S, D, N, H = 1024, 2048, 512, 4, 256, 512
FLOPS = 2 * K * H * S * 2 + 2 * H * N * S

F32 = mybir.dt.float32
BF16 = mybir.dt.bfloat16
I32 = mybir.dt.int32
U32 = mybir.dt.uint32
U16 = mybir.dt.uint16
U8 = mybir.dt.uint8
FP8X4 = mybir.dt.float8_e4m3fn_x4
ALU = mybir.AluOpType
ACT = mybir.ActivationFunctionType

P = 128
PACK = 4
PASSES = K // (P * PACK)
EXP_CAP = math.exp(32.0)
SHIFT = 0.4
EXP_SHIFT = math.exp(SHIFT)
DIV = 256


def tile_picked_ycachep_adm_p_kernel(
    tc, x_words, x_scales, w1, w2, unit, w3, offs, pf, out
):
    nc = tc.nc
    with ExitStack() as ctx:
        keep = ctx.enter_context(tc.tile_pool(name="keep", bufs=1))
        psum = ctx.enter_context(tc.psum_pool(name="psum", bufs=1))

        def sb(name, shape, dtype, tag=None):
            return keep.tile(shape, dtype, name=name, tag=tag or name, align_bytes=64)

        offs_sb = keep.tile([P, S // 16], U16, name="offs_sb")
        pf_sb = keep.tile([P, S // 16], U16, name="pf_sb")
        nc.sync.dma_start(offs_sb[:], offs)
        nc.sync.dma_start(pf_sb[:], pf)
        unit_sb = sb("unit_sb", [P, PACK], F32)
        nc.sync.dma_start(unit_sb[:], unit.rearrange("(p t) one -> p (t one)", t=PACK))

        xs_table = sb("xs_table", [P, T], U8)
        nc.gpsimd.memset(xs_table[:].bitcast(I32), 0)
        for q in range(4):
            nc.scalar.dma_start(
                xs_table[32 * q : 32 * q + 4 * PASSES, :].bitcast(I32),
                x_scales[:, 4 * q : 4 * q + 4, :].bitcast(I32),
            )

        def load_weight(name, w, o, c0, c1):
            raw = sb(f"{name}_raw{o}_{c0}", [P, PACK, c1 - c0], F32)
            nc.sync.dma_start(raw[:], w[512 * o : 512 * (o + 1), c0:c1].rearrange("(p j) c -> p j c", j=PACK))
            return raw

        def load_words(o):
            tab = sb(f"xw_table{o}", [P, T], I32)
            nc.sync.dma_start(tab[:], x_words[o].rearrange("p c r -> p (c r)").bitcast(I32))
            return tab

        w1a = [load_weight("w1", w1, 0, 0, H)]
        w2a = [load_weight("w2", w2, 0, 0, H)]
        xw_table = [load_words(o) for o in range(PASSES)]
        w1b = [load_weight("w1", w1, 1, c, c + H // 2) for c in (0, H // 2)]
        w2b = [load_weight("w2", w2, 1, c, c + H // 2) for c in (0, H // 2)]
        w3_raw = load_weight("w3", w3, 0, 0, N)

        def round_first_weight(name, raws, copy):
            grouped = sb(f"{name}_bf", [P, PACK, P, PACK], BF16)
            width = P // len(raws)
            for i, raw in enumerate(raws):
                copy(
                    grouped[:, :, width * i : width * (i + 1), :].rearrange("p t m j -> p m j t"),
                    raw[:].rearrange("p j (m t) -> p m j t", t=PACK),
                )
            return grouped

        def quantize_first_weight(name, grouped, pieces):
            codes = sb(f"{name}_codes", [P, H], U32)
            scales = sb(f"{name}_scales", [P, H], U8)
            flat = grouped[:].rearrange("p t m j -> p (t m j)")
            width = H // pieces
            for i in range(pieces):
                cols = slice(width * i, width * (i + 1))
                nc.vector.quantize_mx(
                    out=codes[:, cols].bitcast(FP8X4),
                    scales=scales[:, cols],
                    in_=flat[:, PACK * width * i : PACK * width * (i + 1)],
                )
            return codes, scales

        def gather_words(o):
            g = sb(f"xw{o}", [P, S], U32)
            nc.vector.tensor_copy(g[:], xw_table[o][:].bitcast(U32).indirect(offs_sb[:]))
            return g

        rc = [psum.tile([P, S], F32, name=f"rc{t}", tag=f"rc{t}") for t in range(PACK)]
        fr = [psum.tile([P, S], F32, name=f"fr{t}", tag=f"fr{t}") for t in range(PACK)]

        def first_pass(banks, wq, o):
            for t in range(PACK):
                cols = slice(P * t, P * (t + 1))
                nc.tensor.matmul_mx(
                    out=banks[t][:],
                    lhsT=wq[0][:, cols].bitcast(FP8X4),
                    lhsT_scale=wq[1][:, cols],
                    rhs=xw[o][:].bitcast(FP8X4),
                    rhs_scale=xs[4 * o : P, :],
                    start=(o == 0),
                    stop=(o == PASSES - 1),
                )

        xs = sb("xs", [P, S], U8)
        nc.vector.tensor_copy(xs[:], xs_table[:].indirect(offs_sb[:]))
        w1a_q = quantize_first_weight("w1a", round_first_weight("w1a", w1a, nc.scalar.copy), 1)
        w2a_q = quantize_first_weight("w2a", round_first_weight("w2a", w2a, nc.scalar.copy), 1)
        xw = [gather_words(0)]
        first_pass(rc, w1a_q, 0)
        first_pass(fr, w2a_q, 0)
        xw.append(gather_words(1))
        w1b_q = quantize_first_weight("w1b", round_first_weight("w1b", w1b, nc.vector.tensor_copy), PACK)
        first_pass(rc, w1b_q, 1)
        w2b_q = quantize_first_weight("w2b", round_first_weight("w2b", w2b, nc.vector.tensor_copy), PACK)
        first_pass(fr, w2b_q, 1)

        def plane(tile, t):
            return tile[:, S * t : S * (t + 1)]

        e_rc = sb("e_rc", [P, PACK * S], F32)
        ec_rc = sb("ec_rc", [P, PACK * S], F32, tag="w2b_bf")
        for t in range(PACK):
            nc.scalar.activation(plane(e_rc, t), rc[t][:], ACT.Exp)
        e_fr = sb("e_fr", [P, PACK * S], F32, tag="before_ln")
        ec_fr = sb("ec_fr", [P, PACK * S], F32)
        for t in range(PACK):
            nc.scalar.activation(plane(e_fr, t), fr[t][:], ACT.Exp)
        nc.vector.tensor_scalar_min(ec_rc[:], e_rc[:], EXP_CAP)
        for t in range(PACK):
            nc.vector.tensor_scalar_min(plane(ec_fr, t), plane(e_fr, t), EXP_CAP)

        den_head = sb("den_head", [P, DIV], F32)
        logs = sb("logs", [P, 2 * PACK * S], F32, tag="before_ln")
        recy = sb("recy", [P, PACK * S], F32, tag="before_exp")
        freq = sb("freq", [P, PACK * S], F32)
        for t in range(PACK):
            nc.scalar.activation(plane(logs, t), plane(ec_rc, t), ACT.Ln, scale=EXP_SHIFT, bias=EXP_SHIFT)
            if t == 0:
                nc.vector.scalar_tensor_tensor(den_head[:], rc[0][:, :DIV], SHIFT, logs[:, :DIV], ALU.add, ALU.max)
            lo = DIV if t == 0 else 0
            nc.vector.scalar_tensor_tensor(
                plane(recy, t)[:, lo:], rc[t][:, lo:], SHIFT, plane(logs, t)[:, lo:], ALU.add, ALU.max
            )
        for t in range(PACK):
            nc.scalar.activation(plane(logs, PACK + t), plane(ec_fr, t), ACT.Ln, bias=1.0)
            nc.vector.tensor_tensor(plane(freq, t), fr[t][:], plane(logs, PACK + t), ALU.max)
        l_den = sb("l_den", [P, PACK * S], F32)
        for t in range(PACK):
            lo = DIV if t == 0 else 0
            nc.scalar.activation(plane(l_den, t)[:, lo:], plane(recy, t)[:, lo:], ACT.Ln)
        inv_head = sb("inv_head", [P, DIV], F32, tag="before_ln")
        nc.vector.reciprocal(inv_head[:], den_head[:])

        w3_bf = sb("w3_bf", [P, N, PACK], BF16)
        nc.vector.tensor_copy(w3_bf[:], w3_raw[:].rearrange("p j n -> p n j"))
        w3_codes = sb("w3_codes", [P, N], U32)
        w3_scales = sb("w3_scales", [P, N], U8)
        nc.vector.quantize_mx(
            out=w3_codes[:].bitcast(FP8X4), scales=w3_scales[:], in_=w3_bf[:].rearrange("p n j -> p (n j)")
        )
        half_unit = sb("half_unit", [P, PACK], F32)
        nc.vector.tensor_scalar_mul(half_unit[:], unit_sb[:], 0.5)

        inv = sb("inv", [P, PACK * S], F32, tag="before_exp")
        upf_u = sb("upf_u", [P, PACK, S], F32)
        lost = sb("lost", [P, PACK, S], F32)
        util, upf, pairs, vict, diff, th, gap = {}, {}, {}, {}, {}, {}, {}

        def reciprocal(t):
            lo = DIV if t == 0 else 0
            nc.scalar.activation(plane(inv, t)[:, lo:], plane(l_den, t)[:, lo:], ACT.Exp, scale=-1.0)

        def utility(t):
            util[t] = sb(f"util{t}", [P, S], F32)
            lo = DIV if t == 0 else 0
            if t == 0:
                nc.vector.tensor_tensor(util[t][:, :DIV], freq[:, :DIV], inv_head[:], ALU.mult)
            nc.vector.tensor_tensor(util[t][:, lo:], plane(freq, t)[:, lo:], plane(inv, t)[:, lo:], ALU.mult)

        def fetch(t):
            upf[t] = sb(f"upf{t}", [P, S], F32)
            for h in range(2):
                nc.scalar.activation(
                    upf[t][:, 256 * h : 256 * (h + 1)], util[t][:].indirect(pf_sb[:, 16 * h : 16 * (h + 1)]), ACT.Copy
                )

        def pair_min(t):
            pairs[t] = sb(f"pairs{t}", [P, S // 2], F32)
            uv = util[t][:].rearrange("p (v e) -> p v e", e=2)
            nc.vector.tensor_tensor(pairs[t][:], uv[:, :, 0], uv[:, :, 1], ALU.min)

        def victim(t):
            low = sb(f"low{t}", [P, S // D], F32)
            pv = pairs[t][:].rearrange("p (v e) -> p v e", e=2)
            nc.vector.tensor_tensor(low[:], pv[:, :, 0], pv[:, :, 1], ALU.min)
            vict[t] = sb(f"vict{t}", [P, S // D], F32)
            nc.scalar.activation(vict[t][:], low[:], ACT.Copy, scale=half_unit[:, t : t + 1])

        def difference(t):
            diff[t] = sb(f"diff{t}", [P, S], F32)
            nc.vector.tensor_tensor(diff[t][:], upf[t][:], util[t][:], ALU.subtract)

        def gate(t):
            th[t] = sb(f"th{t}", [P, S], F32)
            nc.scalar.activation(th[t][:], diff[t][:], ACT.Tanh, scale=0.75)

        def gapf(t):
            gap[t] = sb(f"gap{t}", [P, S // D, D], F32)
            nc.vector.scalar_tensor_tensor(
                gap[t][:],
                diff[t][:].rearrange("p (v d) -> p v d", d=D),
                half_unit[:, t : t + 1],
                vict[t][:].unsqueeze(2).to_broadcast([P, S // D, D]),
                ALU.mult,
                ALU.add,
            )

        def scale_upf(t):
            nc.scalar.activation(upf_u[:, t, :], upf[t][:], ACT.Copy, scale=unit_sb[:, t : t + 1])

        def loss(t, cols):
            nc.vector.scalar_tensor_tensor(
                lost[:, t, cols], th[t][:, cols], -1.0, gap[t][:].rearrange("p v d -> p (v d)")[:, cols], ALU.add, ALU.mult
            )

        chunks = [slice(0, 256), slice(256, 384), slice(384, 512)]
        reciprocal(0)
        reciprocal(1)
        utility(0)
        fetch(0)
        for t in range(PACK):
            if t + 2 < PACK:
                reciprocal(t + 2)
            if t + 1 < PACK:
                utility(t + 1)
                fetch(t + 1)
            pair_min(t)
            if t > 0:
                gapf(t - 1)
            victim(t)
            if t > 1:
                loss(t - 2, slice(0, S))
            difference(t)
            gate(t)
            if t > 0:
                scale_upf(t - 1)
        loss(PACK - 2, slice(0, S))
        gapf(PACK - 1)
        scale_upf(PACK - 1)
        loss(PACK - 1, slice(0, 256))
        loss(PACK - 1, slice(256, 512))

        hid = {}

        def combine(c):
            cols = chunks[c]
            hid[c] = sb(f"hid_bf{c}", [P, cols.stop - cols.start, PACK], BF16)
            nc.vector.tensor_tensor(
                hid[c][:].rearrange("p (c i) t -> p c t i", i=4),
                upf_u[:, :, cols].rearrange("p t (c i) -> p c t i", i=4),
                lost[:, :, cols].rearrange("p t (c i) -> p c t i", i=4),
                ALU.add,
            )

        def finish(c):
            cols = chunks[c]
            width = cols.stop - cols.start
            h_codes = sb(f"h_codes{c}", [P, width], U32)
            h_scales = sb(f"h_scales{c}", [P, width], U8)
            nc.vector.quantize_mx(
                out=h_codes[:].bitcast(FP8X4), scales=h_scales[:], in_=hid[c][:].rearrange("p j t -> p (j t)")
            )
            for m in range(N // P):
                rows = slice(P * m, P * (m + 1))
                acc = psum.tile([P, width], F32, name=f"o{c}{m}", tag=("rc", "fr")[m] + str(c))
                nc.tensor.matmul_mx(
                    out=acc[:],
                    lhsT=w3_codes[:, rows].bitcast(FP8X4),
                    lhsT_scale=w3_scales[:, rows],
                    rhs=h_codes[:].bitcast(FP8X4),
                    rhs_scale=h_scales[:],
                    start=True,
                    stop=True,
                )
                res = sb(f"res{c}{m}", [P, width], F32)
                if c == len(chunks) - 1 and m == 1:
                    nc.vector.tensor_copy(res[:], acc[:])
                    nc.sync.dma_start(out[rows, cols], res[:])
                else:
                    nc.scalar.copy(res[:], acc[:])
                    (nc.scalar if c == len(chunks) - 1 else nc.sync).dma_start(out[rows, cols], res[:])

        combine(0)
        for c in range(len(chunks)):
            if c + 1 < len(chunks):
                combine(c + 1)
            finish(c)
